import numpy as np
import ml_dtypes


def mxq(x, axis, fmt="e4m3"):
    dtype, down = {"e4m3": (ml_dtypes.float8_e4m3fn, 7), "e5m2": (ml_dtypes.float8_e5m2, 14)}[fmt]
    v = np.moveaxis(np.asarray(x, np.float32).astype(ml_dtypes.bfloat16).astype(np.float64), axis, -1)
    blocks = v.reshape(v.shape[:-1] + (-1, 32))
    amax = np.abs(blocks).max(-1, keepdims=True)
    byte = np.maximum(np.where(amax > 0, np.frexp(amax)[1] - 1 + 127, 0) - down, 1)
    scale = np.exp2(byte - 127.0)
    codes = (blocks / scale).astype(np.float32).astype(dtype).astype(np.float64)
    return np.moveaxis((codes * scale).reshape(v.shape), -1, axis)


WIDE = False


def mx_kscale(k):
    if not WIDE:
        return np.ones(k)
    levels = np.array([10, -10, 5, -5, 0])
    if k % 512:
        return np.exp2(np.random.permutation(np.resize(levels, k // 32))).repeat(32)
    a = np.empty((k // 512, 16))
    for p in range(k // 512):
        a[p, :8] = np.random.permutation(np.resize(levels, 8))
        for g in range(8):
            far = levels[np.abs(levels - a[p, g]) >= 10]
            a[p, g + 8] = far[np.random.randint(len(far))]
    return np.exp2(a.ravel()).repeat(32)


def f64(x):
    return np.asarray(x).astype(np.float64)


def striped(idx):
    return np.tile(idx.reshape(-1, 16).T, (8, 1)).astype(np.uint16)


def unstriped(offs):
    return offs[:16].T.reshape(-1).astype(np.int64)


def striped8(idx):
    return np.concatenate([x.reshape(-1, 16).T for x in idx]).astype(np.uint16)


def runs(offs, k):
    lists = np.stack([offs[16 * r : 16 * r + 16].T.reshape(-1) for r in range(8)]).astype(np.int64)
    return lists[np.arange(k) % 512 // 64]


def pack_weight(w):
    k, n = w.shape
    w = f64(np.asarray(w, np.float32).astype(ml_dtypes.bfloat16)).reshape(k // 32, 32, n)
    amax = np.abs(w).max(1)
    byte = np.clip(np.where(amax > 0, np.frexp(amax)[1] - 1 + 127 - 7, 1), 1, 254)
    scaled = (w * np.exp2(127.0 - byte)[:, None, :]).reshape(k, n).astype(np.float32)
    words = np.ascontiguousarray(scaled.reshape(k // 512, 128, 4, n).transpose(0, 1, 3, 2)).astype(ml_dtypes.float8_e4m3fn).view(np.uint8)
    return words, np.ascontiguousarray(byte.astype(np.uint8).reshape(k // 512, 16, n))


def unpack_weight(words, scales):
    g, p, n, _ = words.shape
    vals = np.ascontiguousarray(words).view(ml_dtypes.float8_e4m3fn).astype(np.float64) * np.repeat(np.exp2(scales.astype(np.float64) - 127.0), 8, axis=1)[..., None]
    return vals.transpose(0, 1, 3, 2).reshape(g * 512, n)


K, T, S, H, J, G = 512, 2048, 512, 512, 512, 2048


def setup_inputs():
    n = np.random.standard_normal
    s = mx_kscale(K)[:, None]
    packed_xT = pack_weight(n((K, T)) * s)
    packed_dT = pack_weight(n((K, G)) / s)
    return {
        "x_words": packed_xT[0],
        "x_scales": packed_xT[1],
        "w1": (n((K, H)) / np.sqrt(K) / s).astype(np.float32),
        "tab": n((H, J)).astype(np.float32),
        "gs": (np.random.uniform(0.5, 1.5, (K, 1)) * s).astype(np.float32),
        "d_words": packed_dT[0],
        "d_scales": packed_dT[1],
        "offs": striped(np.random.permutation(T)[:S]),
        "n1": striped8(np.random.randint(0, J, (8, S))),
        "n2": striped8(np.stack([np.random.permutation(S) for _ in range(8)])),
        "k1": striped8(np.random.randint(0, G, (8, H))),
        "n3": striped8(np.stack([np.random.permutation(S) for _ in range(8)])),
        "n4": striped8(np.stack([np.random.permutation(S) for _ in range(8)])),
        "n5": striped8(np.stack([np.random.permutation(S) for _ in range(8)])),
    }


def reference(x_words, x_scales, w1, tab, gs, d_words, d_scales, offs, n1, n2, k1, n3, n4, n5):
    d_k1 = unpack_weight(d_words, d_scales)[np.arange(K)[:, None], runs(k1, K)]
    xq = unpack_weight(x_words, x_scales)[:, unstriped(offs)]
    y = mxq(f64(w1), 0, "e4m3").T @ xq
    z = f64(gs) * (np.maximum(y + f64(tab)[np.arange(H)[:, None], runs(n1, H)], y[np.arange(H)[:, None], runs(n2, H)]))
    h = 0.0625 * ((d_k1.T @ mxq(z, 0, "e4m3")))
    return np.maximum(h, h[np.arange(H)[:, None], runs(n3, H)]) - (np.maximum(h[np.arange(H)[:, None], runs(n4, H)], h[np.arange(H)[:, None], runs(n5, H)]))

@@ -1,0 +1,204 @@
+from contextlib import ExitStack
+
+import concourse.mybir as mybir
+
+K, T, S, H, J, G = 512, 2048, 512, 512, 512, 2048
+FLOPS = 2 * K * H * S + 2 * K * H * S
+
+F32 = mybir.dt.float32
+BF16 = mybir.dt.bfloat16
+I32 = mybir.dt.int32
+U32 = mybir.dt.uint32
+U16 = mybir.dt.uint16
+U8 = mybir.dt.uint8
+FP8X4 = mybir.dt.float8_e4m3fn_x4
+ALU = mybir.AluOpType
+COPY = mybir.ActivationFunctionType.Copy
+
+P = 128
+PACK = 4
+HALF = S // 2
+LIST_COLS = S // 16
+PREGATHERED = 2
+
+
+def tile_picked_densekindmix_none_p_kernel(
+    tc, x_words, x_scales, w1, tab, gs, d_words, d_scales, offs, n1, n2, k1, n3, n4, n5, out
+):
+    nc = tc.nc
+    with ExitStack() as ctx:
+        keep = ctx.enter_context(tc.tile_pool(name="keep", bufs=1))
+        psum = ctx.enter_context(tc.psum_pool(name="psum", bufs=1))
+
+        def new(shape, dtype, name, tag=None):
+            return keep.tile(shape, dtype, name=name, tag=tag or name, align_bytes=64)
+
+        def load_list(src, name):
+            tile = new([P, LIST_COLS], U16, name)
+            nc.sync.dma_start(tile[:], src)
+            return tile
+
+        def half_cols(c):
+            return slice(c * HALF, (c + 1) * HALF)
+
+        def half_list(tile, c):
+            return tile[:, c * LIST_COLS // 2 : (c + 1) * LIST_COLS // 2]
+
+        ds_table = new([P, G], U8, "ds_table")
+        xs_table = new([P, T], U8, "xs_table")
+        ds_plane = new([P, H], U8, "ds_plane")
+        nc.vector.memset(ds_table[:].bitcast(I32), 0)
+        nc.vector.memset(xs_table[:].bitcast(I32), 0)
+        nc.vector.memset(ds_plane[:].bitcast(I32), 0)
+        hneg = [new([P, 2 * S], F32, "hneg%d" % t) for t in range(PACK)]
+        for t in range(PACK):
+            nc.vector.memset(hneg[t][:, S:], 0.0)
+
+        tab_rows = tab.rearrange("(p t) j -> p t j", t=PACK)
+        tab_t = [new([P, J], F32, "tab%d" % t) for t in range(PACK)]
+        w_rows = w1.rearrange("(p j) c -> p j c", j=PACK)
+        w_raw = [new([P, PACK, H // 2], F32, "w_raw%d" % u) for u in range(2)]
+        xw_table = new([P, T], I32, "xw_table")
+        dw_table = new([P, G], I32, "dw_table")
+        gain = new([P, PACK], F32, "gain")
+
+        k1_t = load_list(k1, "k1_t")
+        nc.sync.dma_start(ds_table[0:P:8, :].bitcast(I32), d_scales[0].bitcast(I32))
+        n1_t = load_list(n1, "n1_t")
+        nc.sync.dma_start(tab_t[0][:], tab_rows[:, 0, :])
+        for u in range(2):
+            nc.sync.dma_start(w_raw[u][:], w_rows[:, :, u * H // 2 : (u + 1) * H // 2])
+        nc.sync.dma_start(xw_table[:], x_words[0].rearrange("p n t -> p (n t)").bitcast(I32))
+        offs_t = load_list(offs, "offs_t")
+        for q in range(4):
+            nc.scalar.dma_start(
+                xs_table[32 * q : 32 * q + 4, :].bitcast(I32), x_scales[0, 4 * q : 4 * q + 4, :].bitcast(I32)
+            )
+        nc.sync.dma_start(tab_t[1][:], tab_rows[:, 1, :])
+        n2_t = load_list(n2, "n2_t")
+        nc.sync.dma_start(gain[:], gs.rearrange("(p t) o -> p (t o)", t=PACK))
+        for t in range(2, PACK):
+            nc.sync.dma_start(tab_t[t][:], tab_rows[:, t, :])
+        nc.sync.dma_start(dw_table[:], d_words[0].rearrange("p n t -> p (n t)").bitcast(I32))
+        n3_t = load_list(n3, "n3_t")
+        n4_t = load_list(n4, "n4_t")
+        n5_t = load_list(n5, "n5_t")
+
+        ds_picked = new([P, H], U8, "ds_picked")
+        nc.vector.tensor_copy(ds_picked[:], ds_table[:].indirect(k1_t[:]))
+        ds_dealt = new([P, H], U8, "ds_dealt")
+        nc.vector.tensor_copy(
+            ds_dealt[:].bitcast(I32).rearrange("p (t a) -> p t a", t=PACK),
+            ds_picked[:].bitcast(I32).rearrange("p (a t) -> p t a", t=PACK),
+        )
+        for q in range(4):
+            nc.gpsimd.dma_start(
+                ds_plane[32 * q : 32 * q + 4, :].bitcast(I32), ds_dealt[32 * q : 32 * q + 32 : 8, :].bitcast(I32)
+            )
+
+        tab_picked = [new([P, S], F32, "tab_picked%d" % t) for t in range(PREGATHERED)]
+
+        def pregather(t):
+            for c in range(2):
+                nc.vector.tensor_copy(tab_picked[t][:, half_cols(c)], tab_t[t][:].indirect(half_list(n1_t, c)))
+
+        pregather(0)
+
+        xs_picked = new([P, S], U8, "xs_picked")
+        nc.vector.tensor_copy(xs_picked[:], xs_table[:].indirect(offs_t[:]))
+
+        w_bf = new([P, H * PACK], BF16, "w_bf")
+        w_dealt = w_bf[:].rearrange("p (t m j) -> p m t j", t=PACK, j=PACK)
+        for u in range(2):
+            nc.scalar.copy(
+                w_dealt[:, u * P // 2 : (u + 1) * P // 2, :, :],
+                w_raw[u][:].rearrange("p j (m t) -> p m t j", t=PACK),
+            )
+        w_codes = new([P, H], U32, "w_codes")
+        w_plane = new([P, H], U8, "w_plane")
+        nc.vector.quantize_mx(out=w_codes[:].bitcast(FP8X4), scales=w_plane[:], in_=w_bf[:])
+
+        xw_picked = new([P, S], U32, "xw_picked")
+        nc.vector.tensor_copy(xw_picked[:], xw_table[:].bitcast(U32).indirect(offs_t[:]))
+        pregather(1)
+
+        y = []
+        for t in range(PACK):
+            cols = slice(t * P, (t + 1) * P)
+            acc = psum.tile([P, S], F32, name="y_acc%d" % t, tag="bank%d" % t)
+            nc.tensor.matmul_mx(
+                out=acc[:],
+                lhsT=w_codes[:, cols].bitcast(FP8X4),
+                lhsT_scale=w_plane[:, cols],
+                rhs=xw_picked[:].bitcast(FP8X4),
+                rhs_scale=xs_picked[:],
+                start=True,
+                stop=True,
+            )
+            y_t = new([P, S], F32, "y%d" % t)
+            nc.scalar.copy(y_t[:], acc[:])
+            y.append(y_t)
+
+        z_bf = [new([P, HALF, PACK], BF16, "z_bf%d" % c) for c in range(2)]
+        for t in range(PACK):
+            for c in range(2):
+                own = new([P, HALF], F32, "own%d_%d" % (t, c))
+                if t < PREGATHERED:
+                    nc.vector.tensor_tensor(own[:], tab_picked[t][:, half_cols(c)], y[t][:, half_cols(c)], ALU.add)
+                else:
+                    nc.vector.tensor_tensor(
+                        own[:], tab_t[t][:].indirect(half_list(n1_t, c)), y[t][:, half_cols(c)], ALU.add
+                    )
+                other = new([P, HALF], F32, "other%d_%d" % (t, c))
+                nc.vector.tensor_copy(other[:], y[t][:].indirect(half_list(n2_t, c)))
+                larger = new([P, HALF], F32, "larger%d_%d" % (t, c))
+                nc.vector.tensor_tensor(larger[:], own[:], other[:], ALU.max)
+                nc.scalar.activation(z_bf[c][:, :, t], larger[:], COPY, scale=gain[:, t : t + 1])
+
+        dw_picked = new([P, H], U32, "dw_picked", tag="other%d_%d" % (PACK - 1, 1))
+        nc.vector.tensor_copy(dw_picked[:], dw_table[:].bitcast(U32).indirect(k1_t[:]))
+        dw_dealt = new([P, H], U32, "dw_dealt")
+        nc.vector.tensor_copy(
+            dw_dealt[:].rearrange("p (t a b) -> p t a b", t=PACK, b=PACK),
+            dw_picked[:].rearrange("p (a t b) -> p t a b", t=PACK, b=PACK),
+        )
+
+        z_codes = [new([P, HALF], U32, "z_codes%d" % c) for c in range(2)]
+        z_plane = [new([P, HALF], U8, "z_plane%d" % c) for c in range(2)]
+        for c in range(2):
+            nc.vector.quantize_mx(
+                out=z_codes[c][:].bitcast(FP8X4), scales=z_plane[c][:], in_=z_bf[c][:].rearrange("p s t -> p (s t)")
+            )
+
+        for t in range(PACK):
+            cols = slice(t * P, (t + 1) * P)
+            for c in range(2):
+                acc = psum.tile([P, HALF], F32, name="h_acc%d_%d" % (t, c), tag="bank%d" % (PACK * (1 - c) + t))
+                nc.tensor.matmul_mx(
+                    out=acc[:],
+                    lhsT=dw_dealt[:, cols].bitcast(FP8X4),
+                    lhsT_scale=ds_plane[:, cols],
+                    rhs=z_codes[c][:].bitcast(FP8X4),
+                    rhs_scale=z_plane[c][:],
+                    start=True,
+                    stop=True,
+                )
+                nc.scalar.activation(hneg[t][:, half_cols(c)], acc[:], COPY, scale=-0.0625)
+
+        out_rows = out.rearrange("(a t b) s -> t a b s", t=PACK, b=PACK)
+        for t in range(PACK):
+            pieces = [(0, S)] if t < PACK - 1 else [(0, HALF), (HALF, S)]
+            for lo, hi in pieces:
+                n = hi - lo
+                lst = slice(lo // 16, hi // 16)
+                at3 = new([P, n], F32, "at3_%d_%d" % (t, lo))
+                nc.vector.tensor_copy(at3[:], hneg[t][:].indirect(n3_t[:, lst]))
+                near = new([P, n], F32, "near_%d_%d" % (t, lo))
+                nc.vector.tensor_tensor(near[:], hneg[t][:, lo:hi], at3[:], ALU.min)
+                via4 = new([P, n], F32, "via4_%d_%d" % (t, lo))
+                nc.vector.tensor_tensor(via4[:], hneg[t][:].indirect(n4_t[:, lst]), near[:], ALU.subtract)
+                via5 = new([P, n], F32, "via5_%d_%d" % (t, lo))
+                nc.vector.tensor_tensor(via5[:], hneg[t][:].indirect(n5_t[:, lst]), near[:], ALU.subtract)
+                res = new([P, n], F32, "res_%d_%d" % (t, lo))
+                nc.vector.tensor_tensor(res[:], via4[:], via5[:], ALU.min)
+                nc.sync.dma_start(out_rows[t][:, :, lo:hi], res[:])

@@ -55,37 +55,46 @@ def tile_picked_densekindmix_none_p_kernel(
             nc.vector.memset(hneg[t][:, S:], 0.0)
 
         tab_rows = tab.rearrange("(p t) j -> p t j", t=PACK)
-        tab_t = [new([P, J], F32, "tab%d" % t) for t in range(PACK)]
-        w_rows = w1.rearrange("(p j) c -> p j c", j=PACK)
-        w_raw = [new([P, PACK, H // 2], F32, "w_raw%d" % u) for u in range(2)]
+        w_raw = new([P, PACK, H], F32, "w_raw")
         xw_table = new([P, T], I32, "xw_table")
-        dw_table = new([P, G], I32, "dw_table")
         gain = new([P, PACK], F32, "gain")
 
-        k1_t = load_list(k1, "k1_t")
-        nc.sync.dma_start(ds_table[0:P:8, :].bitcast(I32), d_scales[0].bitcast(I32))
+        def load_tab(t, tag):
+            tile = new([P, J], F32, "tab%d" % t, tag=tag)
+            nc.sync.dma_start(tile[:], tab_rows[:, t, :])
+            return tile
+
         n1_t = load_list(n1, "n1_t")
-        nc.sync.dma_start(tab_t[0][:], tab_rows[:, 0, :])
-        for u in range(2):
-            nc.sync.dma_start(w_raw[u][:], w_rows[:, :, u * H // 2 : (u + 1) * H // 2])
-        nc.sync.dma_start(xw_table[:], x_words[0].rearrange("p n t -> p (n t)").bitcast(I32))
+        tab_t = [load_tab(0, "tab0")]
         offs_t = load_list(offs, "offs_t")
+        k1_t = load_list(k1, "k1_t")
+        n2_t = load_list(n2, "n2_t")
+        n3_t = load_list(n3, "n3_t")
+        n4_t = load_list(n4, "n4_t")
+        nc.sync.dma_start(w_raw[:], w1.rearrange("(p j) c -> p j c", j=PACK))
+        nc.sync.dma_start(xw_table[:], x_words[0].rearrange("p n t -> p (n t)").bitcast(I32))
+        n5_t = load_list(n5, "n5_t")
+        nc.scalar.dma_start(ds_table[0:P:8, :].bitcast(I32), d_scales[0].bitcast(I32))
         for q in range(4):
             nc.scalar.dma_start(
                 xs_table[32 * q : 32 * q + 4, :].bitcast(I32), x_scales[0, 4 * q : 4 * q + 4, :].bitcast(I32)
             )
-        nc.sync.dma_start(tab_t[1][:], tab_rows[:, 1, :])
-        n2_t = load_list(n2, "n2_t")
-        nc.sync.dma_start(gain[:], gs.rearrange("(p t) o -> p (t o)", t=PACK))
-        for t in range(2, PACK):
-            nc.sync.dma_start(tab_t[t][:], tab_rows[:, t, :])
-        nc.sync.dma_start(dw_table[:], d_words[0].rearrange("p n t -> p (n t)").bitcast(I32))
-        n3_t = load_list(n3, "n3_t")
-        n4_t = load_list(n4, "n4_t")
-        n5_t = load_list(n5, "n5_t")
+        nc.gpsimd.dma_start(gain[:], gs.rearrange("(p t) o -> p (t o)", t=PACK))
+
+        tab_picked = []
+
+        def pregather(t, tag):
+            tab_picked.append(new([P, S], F32, "tab_picked%d" % t, tag=tag))
+            for c in range(2):
+                nc.vector.tensor_copy(tab_picked[t][:, half_cols(c)], tab_t[t][:].indirect(half_list(n1_t, c)))
+
+        pregather(0, "tab_picked0")
+        tab_t.append(load_tab(1, "tab0"))
 
         ds_picked = new([P, H], U8, "ds_picked")
         nc.vector.tensor_copy(ds_picked[:], ds_table[:].indirect(k1_t[:]))
+        xs_picked = new([P, S], U8, "xs_picked", tag="ds_table")
+        nc.vector.tensor_copy(xs_picked[:], xs_table[:].indirect(offs_t[:]))
         ds_dealt = new([P, H], U8, "ds_dealt")
         nc.vector.tensor_copy(
             ds_dealt[:].bitcast(I32).rearrange("p (t a) -> p t a", t=PACK),
@@ -96,31 +105,20 @@ def tile_picked_densekindmix_none_p_kernel(
                 ds_plane[32 * q : 32 * q + 4, :].bitcast(I32), ds_dealt[32 * q : 32 * q + 32 : 8, :].bitcast(I32)
             )
 
-        tab_picked = [new([P, S], F32, "tab_picked%d" % t) for t in range(PREGATHERED)]
-
-        def pregather(t):
-            for c in range(2):
-                nc.vector.tensor_copy(tab_picked[t][:, half_cols(c)], tab_t[t][:].indirect(half_list(n1_t, c)))
-
-        pregather(0)
-
-        xs_picked = new([P, S], U8, "xs_picked")
-        nc.vector.tensor_copy(xs_picked[:], xs_table[:].indirect(offs_t[:]))
-
         w_bf = new([P, H * PACK], BF16, "w_bf")
         w_dealt = w_bf[:].rearrange("p (t m j) -> p m t j", t=PACK, j=PACK)
-        for u in range(2):
-            nc.scalar.copy(
-                w_dealt[:, u * P // 2 : (u + 1) * P // 2, :, :],
-                w_raw[u][:].rearrange("p j (m t) -> p m t j", t=PACK),
-            )
-        w_codes = new([P, H], U32, "w_codes")
+        nc.scalar.activation(w_dealt, w_raw[:].rearrange("p j (m t) -> p m t j", t=PACK), COPY)
+        dw_table = new([P, G], I32, "dw_table", tag="w_raw")
+        nc.sync.dma_start(dw_table[:], d_words[0].rearrange("p n t -> p (n t)").bitcast(I32))
+
+        xw_picked = new([P, S], U32, "xw_picked", tag="xs_table")
+        nc.vector.tensor_copy(xw_picked[:], xw_table[:].bitcast(U32).indirect(offs_t[:]))
+
+        w_codes = new([P, H], U32, "w_codes", tag="xw_table")
         w_plane = new([P, H], U8, "w_plane")
         nc.vector.quantize_mx(out=w_codes[:].bitcast(FP8X4), scales=w_plane[:], in_=w_bf[:])
-
-        xw_picked = new([P, S], U32, "xw_picked")
-        nc.vector.tensor_copy(xw_picked[:], xw_table[:].bitcast(U32).indirect(offs_t[:]))
-        pregather(1)
+        pregather(1, "w_bf")
+        tab_t.append(load_tab(2, "tab0"))
 
         y = []
         for t in range(PACK):
@@ -141,34 +139,39 @@ def tile_picked_densekindmix_none_p_kernel(
 
         z_bf = [new([P, HALF, PACK], BF16, "z_bf%d" % c) for c in range(2)]
         for t in range(PACK):
+            own = [new([P, HALF], F32, "own%d_%d" % (t, c)) for c in range(2)]
+            other = [new([P, HALF], F32, "other%d_%d" % (t, c)) for c in range(2)]
+            larger = [new([P, HALF], F32, "larger%d_%d" % (t, c)) for c in range(2)]
             for c in range(2):
-                own = new([P, HALF], F32, "own%d_%d" % (t, c))
-                if t < PREGATHERED:
-                    nc.vector.tensor_tensor(own[:], tab_picked[t][:, half_cols(c)], y[t][:, half_cols(c)], ALU.add)
-                else:
-                    nc.vector.tensor_tensor(
-                        own[:], tab_t[t][:].indirect(half_list(n1_t, c)), y[t][:, half_cols(c)], ALU.add
-                    )
-                other = new([P, HALF], F32, "other%d_%d" % (t, c))
-                nc.vector.tensor_copy(other[:], y[t][:].indirect(half_list(n2_t, c)))
-                larger = new([P, HALF], F32, "larger%d_%d" % (t, c))
-                nc.vector.tensor_tensor(larger[:], own[:], other[:], ALU.max)
-                nc.scalar.activation(z_bf[c][:, :, t], larger[:], COPY, scale=gain[:, t : t + 1])
+                looked_up = (
+                    tab_picked[t][:, half_cols(c)] if t < PREGATHERED else tab_t[t][:].indirect(half_list(n1_t, c))
+                )
+                nc.vector.tensor_tensor(own[c][:], looked_up, y[t][:, half_cols(c)], ALU.add)
+            if t == 0:
+                tab_t.append(load_tab(3, "tab_picked0"))
+            for c in range(2):
+                nc.vector.tensor_copy(other[c][:], y[t][:].indirect(half_list(n2_t, c)))
+            for c in range(2):
+                nc.vector.tensor_tensor(larger[c][:], own[c][:], other[c][:], ALU.max)
+                nc.scalar.activation(z_bf[c][:, :, t], larger[c][:], COPY, scale=gain[:, t : t + 1])
+
+        z_codes = [new([P, HALF], U32, "z_codes%d" % c) for c in range(2)]
+        z_plane = [new([P, HALF], U8, "z_plane%d" % c) for c in range(2)]
+
+        def quantise_z(c):
+            nc.vector.quantize_mx(
+                out=z_codes[c][:].bitcast(FP8X4), scales=z_plane[c][:], in_=z_bf[c][:].rearrange("p s t -> p (s t)")
+            )
 
         dw_picked = new([P, H], U32, "dw_picked", tag="other%d_%d" % (PACK - 1, 1))
         nc.vector.tensor_copy(dw_picked[:], dw_table[:].bitcast(U32).indirect(k1_t[:]))
+        quantise_z(0)
         dw_dealt = new([P, H], U32, "dw_dealt")
         nc.vector.tensor_copy(
             dw_dealt[:].rearrange("p (t a b) -> p t a b", t=PACK, b=PACK),
             dw_picked[:].rearrange("p (a t b) -> p t a b", t=PACK, b=PACK),
         )
-
-        z_codes = [new([P, HALF], U32, "z_codes%d" % c) for c in range(2)]
-        z_plane = [new([P, HALF], U8, "z_plane%d" % c) for c in range(2)]
-        for c in range(2):
-            nc.vector.quantize_mx(
-                out=z_codes[c][:].bitcast(FP8X4), scales=z_plane[c][:], in_=z_bf[c][:].rearrange("p s t -> p (s t)")
-            )
+        quantise_z(1)
 
         for t in range(PACK):
             cols = slice(t * P, (t + 1) * P)
@@ -186,19 +189,29 @@ def tile_picked_densekindmix_none_p_kernel(
                 nc.scalar.activation(hneg[t][:, half_cols(c)], acc[:], COPY, scale=-0.0625)
 
         out_rows = out.rearrange("(a t b) s -> t a b s", t=PACK, b=PACK)
-        for t in range(PACK):
-            pieces = [(0, S)] if t < PACK - 1 else [(0, HALF), (HALF, S)]
-            for lo, hi in pieces:
-                n = hi - lo
-                lst = slice(lo // 16, hi // 16)
-                at3 = new([P, n], F32, "at3_%d_%d" % (t, lo))
-                nc.vector.tensor_copy(at3[:], hneg[t][:].indirect(n3_t[:, lst]))
-                near = new([P, n], F32, "near_%d_%d" % (t, lo))
-                nc.vector.tensor_tensor(near[:], hneg[t][:, lo:hi], at3[:], ALU.min)
-                via4 = new([P, n], F32, "via4_%d_%d" % (t, lo))
-                nc.vector.tensor_tensor(via4[:], hneg[t][:].indirect(n4_t[:, lst]), near[:], ALU.subtract)
-                via5 = new([P, n], F32, "via5_%d_%d" % (t, lo))
-                nc.vector.tensor_tensor(via5[:], hneg[t][:].indirect(n5_t[:, lst]), near[:], ALU.subtract)
-                res = new([P, n], F32, "res_%d_%d" % (t, lo))
-                nc.vector.tensor_tensor(res[:], via4[:], via5[:], ALU.min)
-                nc.sync.dma_start(out_rows[t][:, :, lo:hi], res[:])
+        pairs = [[(0, 0, HALF), (0, HALF, S)], [(1, 0, S), (2, 0, S)], [(3, 0, HALF), (3, HALF, S)]]
+        for pair in pairs:
+            def tiles(name):
+                return [new([P, hi - lo], F32, "%s_%d_%d" % (name, t, lo)) for t, lo, hi in pair]
+
+            def window(u, lists):
+                t, lo, hi = pair[u]
+                return hneg[t][:].indirect(lists[:, lo // 16 : hi // 16])
+
+            at3, near, via4, via5, res = [tiles(name) for name in ("at3", "near", "via4", "via5", "res")]
+
+            def finish(u):
+                t, lo, hi = pair[u]
+                nc.vector.tensor_tensor(res[u][:], via4[u][:], via5[u][:], ALU.min)
+                nc.sync.dma_start(out_rows[t][:, :, lo:hi], res[u][:])
+
+            for u in range(2):
+                nc.vector.tensor_copy(at3[u][:], window(u, n3_t))
+            for u, (t, lo, hi) in enumerate(pair):
+                nc.vector.tensor_tensor(near[u][:], hneg[t][:, lo:hi], at3[u][:], ALU.min)
+            nc.vector.tensor_tensor(via4[0][:], window(0, n4_t), near[0][:], ALU.subtract)
+            nc.vector.tensor_tensor(via5[0][:], window(0, n5_t), near[0][:], ALU.subtract)
+            nc.vector.tensor_tensor(via4[1][:], window(1, n4_t), near[1][:], ALU.subtract)
+            finish(0)
+            nc.vector.tensor_tensor(via5[1][:], window(1, n5_t), near[1][:], ALU.subtract)
+            finish(1)

@@ -1,6 +1,7 @@
 from contextlib import ExitStack
 
 import concourse.mybir as mybir
+from concourse.masks import make_identity
 
 K, T, S, H, J, G = 512, 2048, 512, 512, 512, 2048
 FLOPS = 2 * K * H * S + 2 * K * H * S
@@ -14,12 +15,14 @@ U8 = mybir.dt.uint8
 FP8X4 = mybir.dt.float8_e4m3fn_x4
 ALU = mybir.AluOpType
 COPY = mybir.ActivationFunctionType.Copy
+RELU = mybir.ActivationFunctionType.Relu
 
 P = 128
 PACK = 4
 HALF = S // 2
 LIST_COLS = S // 16
 PREGATHERED = 2
+W_SPLIT = 96
 
 
 def tile_picked_densekindmix_none_p_kernel(
@@ -47,16 +50,16 @@ def tile_picked_densekindmix_none_p_kernel(
         ds_table = new([P, G], U8, "ds_table")
         xs_table = new([P, T], U8, "xs_table")
         ds_plane = new([P, H], U8, "ds_plane")
-        nc.vector.memset(ds_table[:].bitcast(I32), 0)
+        nc.gpsimd.memset(ds_table[:].bitcast(I32), 0)
+        nc.gpsimd.dma_start(ds_table[0:P:8, :].bitcast(I32), d_scales[0].bitcast(I32))
         nc.vector.memset(xs_table[:].bitcast(I32), 0)
         nc.vector.memset(ds_plane[:].bitcast(I32), 0)
         hneg = [new([P, 2 * S], F32, "hneg%d" % t) for t in range(PACK)]
         for t in range(PACK):
-            nc.vector.memset(hneg[t][:, S:], 0.0)
+            (nc.vector if t < 2 else nc.gpsimd).memset(hneg[t][:, S:], 0.0)
 
         tab_rows = tab.rearrange("(p t) j -> p t j", t=PACK)
         w_raw = new([P, PACK, H], F32, "w_raw")
-        xw_table = new([P, T], I32, "xw_table")
         gain = new([P, PACK], F32, "gain")
 
         def load_tab(t, tag):
@@ -65,21 +68,21 @@ def tile_picked_densekindmix_none_p_kernel(
             return tile
 
         n1_t = load_list(n1, "n1_t")
-        tab_t = [load_tab(0, "tab0")]
+        tab_t = [load_tab(t, "tab%d" % t) for t in range(2)]
         offs_t = load_list(offs, "offs_t")
         k1_t = load_list(k1, "k1_t")
         n2_t = load_list(n2, "n2_t")
         n3_t = load_list(n3, "n3_t")
-        n4_t = load_list(n4, "n4_t")
         nc.sync.dma_start(w_raw[:], w1.rearrange("(p j) c -> p j c", j=PACK))
-        nc.sync.dma_start(xw_table[:], x_words[0].rearrange("p n t -> p (n t)").bitcast(I32))
+        n4_t = load_list(n4, "n4_t")
         n5_t = load_list(n5, "n5_t")
-        nc.scalar.dma_start(ds_table[0:P:8, :].bitcast(I32), d_scales[0].bitcast(I32))
         for q in range(4):
-            nc.scalar.dma_start(
+            nc.sync.dma_start(
                 xs_table[32 * q : 32 * q + 4, :].bitcast(I32), x_scales[0, 4 * q : 4 * q + 4, :].bitcast(I32)
             )
         nc.gpsimd.dma_start(gain[:], gs.rearrange("(p t) o -> p (t o)", t=PACK))
+        ident = new([P, P], F32, "ident")
+        make_identity(nc, ident[:])
 
         tab_picked = []
 
@@ -89,36 +92,30 @@ def tile_picked_densekindmix_none_p_kernel(
                 nc.vector.tensor_copy(tab_picked[t][:, half_cols(c)], tab_t[t][:].indirect(half_list(n1_t, c)))
 
         pregather(0, "tab_picked0")
-        tab_t.append(load_tab(1, "tab0"))
+        xw_table = new([P, T], I32, "xw_table", tag="tab0")
+        nc.sync.dma_start(xw_table[:], x_words[0].rearrange("p n t -> p (n t)").bitcast(I32))
 
-        ds_picked = new([P, H], U8, "ds_picked")
-        nc.vector.tensor_copy(ds_picked[:], ds_table[:].indirect(k1_t[:]))
-        xs_picked = new([P, S], U8, "xs_picked", tag="ds_table")
-        nc.vector.tensor_copy(xs_picked[:], xs_table[:].indirect(offs_t[:]))
-        ds_dealt = new([P, H], U8, "ds_dealt")
-        nc.vector.tensor_copy(
-            ds_dealt[:].bitcast(I32).rearrange("p (t a) -> p t a", t=PACK),
-            ds_picked[:].bitcast(I32).rearrange("p (a t) -> p t a", t=PACK),
-        )
-        for q in range(4):
-            nc.gpsimd.dma_start(
-                ds_plane[32 * q : 32 * q + 4, :].bitcast(I32), ds_dealt[32 * q : 32 * q + 32 : 8, :].bitcast(I32)
-            )
-
+        pregather(1, "tab_picked1")
+        tab_t.append(load_tab(2, "tab1"))
         w_bf = new([P, H * PACK], BF16, "w_bf")
         w_dealt = w_bf[:].rearrange("p (t m j) -> p m t j", t=PACK, j=PACK)
-        nc.scalar.activation(w_dealt, w_raw[:].rearrange("p j (m t) -> p m t j", t=PACK), COPY)
+        w_source = w_raw[:].rearrange("p j (m t) -> p m t j", t=PACK)
+        nc.scalar.activation(w_dealt[:, :W_SPLIT], w_source[:, :W_SPLIT], COPY)
+        nc.vector.tensor_copy(w_dealt[:, W_SPLIT:], w_source[:, W_SPLIT:])
         dw_table = new([P, G], I32, "dw_table", tag="w_raw")
         nc.sync.dma_start(dw_table[:], d_words[0].rearrange("p n t -> p (n t)").bitcast(I32))
+        xs_picked = new([P, S], U8, "xs_picked")
+        nc.vector.tensor_copy(xs_picked[:], xs_table[:].indirect(offs_t[:]))
 
-        xw_picked = new([P, S], U32, "xw_picked", tag="xs_table")
-        nc.vector.tensor_copy(xw_picked[:], xw_table[:].bitcast(U32).indirect(offs_t[:]))
-
-        w_codes = new([P, H], U32, "w_codes", tag="xw_table")
+        w_codes = new([P, H], U32, "w_codes", tag="xs_table")
         w_plane = new([P, H], U8, "w_plane")
         nc.vector.quantize_mx(out=w_codes[:].bitcast(FP8X4), scales=w_plane[:], in_=w_bf[:])
-        pregather(1, "w_bf")
-        tab_t.append(load_tab(2, "tab0"))
+
+        xw_picked = new([P, S], U32, "xw_picked", tag="w_bf")
+        nc.vector.tensor_copy(xw_picked[:], xw_table[:].bitcast(U32).indirect(offs_t[:]))
+
+        ds_picked = new([P, H], U8, "ds_picked", tag="tab0")
+        nc.vector.tensor_copy(ds_picked[:], ds_table[:].indirect(k1_t[:]))
 
         y = []
         for t in range(PACK):
@@ -138,80 +135,148 @@ def tile_picked_densekindmix_none_p_kernel(
             y.append(y_t)
 
         z_bf = [new([P, HALF, PACK], BF16, "z_bf%d" % c) for c in range(2)]
-        for t in range(PACK):
-            own = [new([P, HALF], F32, "own%d_%d" % (t, c)) for c in range(2)]
-            other = [new([P, HALF], F32, "other%d_%d" % (t, c)) for c in range(2)]
-            larger = [new([P, HALF], F32, "larger%d_%d" % (t, c)) for c in range(2)]
+        own = [[new([P, HALF], F32, "own%d_%d" % (t, c)) for c in range(2)] for t in range(PACK)]
+        other = [[new([P, HALF], F32, "other%d_%d" % (t, c)) for c in range(2)] for t in range(PACK)]
+
+        def add_kind(t, c):
+            looked_up = tab_picked[t][:, half_cols(c)] if t < PREGATHERED else tab_t[t][:].indirect(half_list(n1_t, c))
+            nc.vector.tensor_tensor(own[t][c][:], looked_up, y[t][:, half_cols(c)], ALU.add)
+
+        def fetch_other(t, c):
+            nc.vector.tensor_copy(other[t][c][:], y[t][:].indirect(half_list(n2_t, c)))
+
+        def weigh_larger(t, c):
+            larger = new([P, HALF], F32, "larger%d_%d" % (t, c))
+            nc.vector.tensor_tensor(larger[:], own[t][c][:], other[t][c][:], ALU.max)
+            nc.scalar.activation(z_bf[c][:, :, t], larger[:], COPY, scale=gain[:, t : t + 1])
+
+        last = PACK - 1
+        for t in range(last):
             for c in range(2):
-                looked_up = (
-                    tab_picked[t][:, half_cols(c)] if t < PREGATHERED else tab_t[t][:].indirect(half_list(n1_t, c))
-                )
-                nc.vector.tensor_tensor(own[c][:], looked_up, y[t][:, half_cols(c)], ALU.add)
+                add_kind(t, c)
             if t == 0:
                 tab_t.append(load_tab(3, "tab_picked0"))
+                ds_dealt = new([P, H], U8, "ds_dealt")
+                nc.vector.tensor_copy(
+                    ds_dealt[:].bitcast(I32).rearrange("p (t a) -> p t a", t=PACK),
+                    ds_picked[:].bitcast(I32).rearrange("p (a t) -> p t a", t=PACK),
+                )
+                for q in range(4):
+                    nc.gpsimd.dma_start(
+                        ds_plane[32 * q : 32 * q + 4, :].bitcast(I32),
+                        ds_dealt[32 * q : 32 * q + 32 : 8, :].bitcast(I32),
+                    )
             for c in range(2):
-                nc.vector.tensor_copy(other[c][:], y[t][:].indirect(half_list(n2_t, c)))
+                fetch_other(t, c)
             for c in range(2):
-                nc.vector.tensor_tensor(larger[c][:], own[c][:], other[c][:], ALU.max)
-                nc.scalar.activation(z_bf[c][:, :, t], larger[c][:], COPY, scale=gain[:, t : t + 1])
+                weigh_larger(t, c)
 
-        z_codes = [new([P, HALF], U32, "z_codes%d" % c) for c in range(2)]
-        z_plane = [new([P, HALF], U8, "z_plane%d" % c) for c in range(2)]
+        z_codes = new([P, S], U32, "z_codes")
+        z_plane = new([P, S], U8, "z_plane")
 
         def quantise_z(c):
             nc.vector.quantize_mx(
-                out=z_codes[c][:].bitcast(FP8X4), scales=z_plane[c][:], in_=z_bf[c][:].rearrange("p s t -> p (s t)")
+                out=z_codes[:, half_cols(c)].bitcast(FP8X4),
+                scales=z_plane[:, half_cols(c)],
+                in_=z_bf[c][:].rearrange("p s t -> p (s t)"),
             )
 
-        dw_picked = new([P, H], U32, "dw_picked", tag="other%d_%d" % (PACK - 1, 1))
-        nc.vector.tensor_copy(dw_picked[:], dw_table[:].bitcast(U32).indirect(k1_t[:]))
+        add_kind(last, 0)
+        fetch_other(last, 0)
+        add_kind(last, 1)
+        weigh_larger(last, 0)
+        fetch_other(last, 1)
+        dw_picked = new([P, H], U32, "dw_picked", tag="other%d_%d" % (last, 0))
+        nc.vector.tensor_copy(dw_picked[:, half_cols(0)], dw_table[:].bitcast(U32).indirect(half_list(k1_t, 0)))
+        weigh_larger(last, 1)
+        nc.vector.tensor_copy(dw_picked[:, half_cols(1)], dw_table[:].bitcast(U32).indirect(half_list(k1_t, 1)))
         quantise_z(0)
-        dw_dealt = new([P, H], U32, "dw_dealt")
-        nc.vector.tensor_copy(
-            dw_dealt[:].rearrange("p (t a b) -> p t a b", t=PACK, b=PACK),
-            dw_picked[:].rearrange("p (a t b) -> p t a b", t=PACK, b=PACK),
-        )
+        dw_dealt = [new([P, P], U32, "dw_dealt0"), new([P, last * P], U32, "dw_dealt1")]
+        dw_source = dw_picked[:].rearrange("p (a t b) -> p t a b", t=PACK, b=PACK)
+        nc.vector.tensor_copy(dw_dealt[0][:].rearrange("p (a b) -> p a b", b=PACK), dw_source[:, 0])
         quantise_z(1)
+        nc.vector.tensor_copy(dw_dealt[1][:].rearrange("p (t a b) -> p t a b", t=last, b=PACK), dw_source[:, 1:])
 
-        for t in range(PACK):
+        def second_product(t, places, bank):
             cols = slice(t * P, (t + 1) * P)
-            for c in range(2):
-                acc = psum.tile([P, HALF], F32, name="h_acc%d_%d" % (t, c), tag="bank%d" % (PACK * (1 - c) + t))
-                nc.tensor.matmul_mx(
-                    out=acc[:],
-                    lhsT=dw_dealt[:, cols].bitcast(FP8X4),
-                    lhsT_scale=ds_plane[:, cols],
-                    rhs=z_codes[c][:].bitcast(FP8X4),
-                    rhs_scale=z_plane[c][:],
-                    start=True,
-                    stop=True,
-                )
-                nc.scalar.activation(hneg[t][:, half_cols(c)], acc[:], COPY, scale=-0.0625)
+            acc = psum.tile([P, places.stop - places.start], F32, name="h_acc%d_%d" % (t, places.start), tag=bank)
+            nc.tensor.matmul_mx(
+                out=acc[:],
+                lhsT=(dw_dealt[1][:, (t - 1) * P : t * P] if t else dw_dealt[0][:]).bitcast(FP8X4),
+                lhsT_scale=ds_plane[:, cols],
+                rhs=z_codes[:, places].bitcast(FP8X4),
+                rhs_scale=z_plane[:, places],
+                start=True,
+                stop=True,
+            )
+            nc.scalar.activation(hneg[t][:, places], acc[:], COPY, scale=-0.0625)
+            return acc
+
+        hpos = [new([P, S], F32, "hpos%d" % t) for t in range(last)]
+        for c in range(2):
+            second_product(0, half_cols(c), "bank%d" % (PACK * (1 - c)))
+        nc.scalar.activation(hpos[0][:], hneg[0][:, :S], COPY, scale=-1.0)
+        for t in range(1, PACK):
+            acc = second_product(t, slice(0, S), "bank%d" % t)
+            if t < last:
+                nc.scalar.activation(hpos[t][:], acc[:], COPY, scale=0.0625)
 
         out_rows = out.rearrange("(a t b) s -> t a b s", t=PACK, b=PACK)
-        pairs = [[(0, 0, HALF), (0, HALF, S)], [(1, 0, S), (2, 0, S)], [(3, 0, HALF), (3, HALF, S)]]
-        for pair in pairs:
-            def tiles(name):
-                return [new([P, hi - lo], F32, "%s_%d_%d" % (name, t, lo)) for t, lo, hi in pair]
 
-            def window(u, lists):
-                t, lo, hi = pair[u]
-                return hneg[t][:].indirect(lists[:, lo // 16 : hi // 16])
+        def turned_sum(terms, name, bank):
+            acc = psum.tile([P, S], F32, name=name, tag=bank)
+            for b in range(S // P):
+                block = slice(b * P, (b + 1) * P)
+                for i, term in enumerate(terms):
+                    nc.tensor.matmul(
+                        acc[:, block], term[:, block], ident[:], start=i == 0, stop=i == len(terms) - 1, is_transpose=True
+                    )
+            result = new([P, S], F32, name + "_sb")
+            nc.scalar.copy(result[:], acc[:])
+            return result
 
-            at3, near, via4, via5, res = [tiles(name) for name in ("at3", "near", "via4", "via5", "res")]
+        def fetch(t, lists, name, lo=0, hi=S):
+            tile = new([P, hi - lo], F32, "%s_%d_%d" % (name, t, lo))
+            nc.vector.tensor_copy(tile[:], hneg[t][:].indirect(lists[:, lo // 16 : hi // 16]))
+            return tile
 
-            def finish(u):
-                t, lo, hi = pair[u]
-                nc.vector.tensor_tensor(res[u][:], via4[u][:], via5[u][:], ALU.min)
-                nc.sync.dma_start(out_rows[t][:, :, lo:hi], res[u][:])
+        def own_less(t, lists, name):
+            tile = new([P, S], F32, "%s_%d" % (name, t))
+            nc.vector.tensor_tensor(tile[:], hneg[t][:].indirect(lists[:]), hpos[t][:], ALU.add)
+            return tile
 
-            for u in range(2):
-                nc.vector.tensor_copy(at3[u][:], window(u, n3_t))
-            for u, (t, lo, hi) in enumerate(pair):
-                nc.vector.tensor_tensor(near[u][:], hneg[t][:, lo:hi], at3[u][:], ALU.min)
-            nc.vector.tensor_tensor(via4[0][:], window(0, n4_t), near[0][:], ALU.subtract)
-            nc.vector.tensor_tensor(via5[0][:], window(0, n5_t), near[0][:], ALU.subtract)
-            nc.vector.tensor_tensor(via4[1][:], window(1, n4_t), near[1][:], ALU.subtract)
-            finish(0)
-            nc.vector.tensor_tensor(via5[1][:], window(1, n5_t), near[1][:], ALU.subtract)
-            finish(1)
+        for t in range(last):
+            if t == 0:
+                at4 = fetch(t, n4_t, "at4")
+                at5 = fetch(t, n5_t, "at5")
+            else:
+                at4 = own_less(t, n4_t, "at4")
+                at5 = own_less(t, n5_t, "at5")
+            drop = own_less(t, n3_t, "drop")
+            far = new([P, S], F32, "far%d" % t)
+            nc.vector.tensor_tensor(far[:], at4[:], at5[:], ALU.min)
+            rise = new([P, S], F32, "rise%d" % t, tag="turned%d_sb" % (t - 1) if t else None)
+            nc.scalar.activation(rise[:], drop[:], RELU, scale=-1.0)
+            turned = turned_sum([far, rise] if t else [hpos[t], far, rise], "turned%d" % t, "bank%d" % (5 + t % 2))
+            nc.sync.dma_start(out_rows[t], turned_sum([turned], "res%d" % t, "bank7")[:])
+
+        at3 = [fetch(last, n3_t, "at3", c * HALF, (c + 1) * HALF) for c in range(2)]
+        near, via4, via5, res = [
+            [new([P, HALF], F32, "%s_last%d" % (name, c)) for c in range(2)] for name in ("near", "via4", "via5", "res")
+        ]
+
+        def less_near(dst, lists, c):
+            nc.vector.tensor_tensor(dst[c][:], hneg[last][:].indirect(half_list(lists, c)), near[c][:], ALU.subtract)
+
+        def finish(c):
+            nc.vector.tensor_tensor(res[c][:], via4[c][:], via5[c][:], ALU.min)
+            nc.sync.dma_start(out_rows[last][:, :, half_cols(c)], res[c][:])
+
+        for c in range(2):
+            nc.vector.tensor_tensor(near[c][:], hneg[last][:, half_cols(c)], at3[c][:], ALU.min)
+        less_near(via4, n4_t, 0)
+        less_near(via5, n5_t, 0)
+        less_near(via4, n4_t, 1)
+        finish(0)
+        less_near(via5, n5_t, 1)
+        finish(1)

@@ -22,7 +22,7 @@ PACK = 4
 HALF = S // 2
 LIST_COLS = S // 16
 PREGATHERED = 2
-W_SPLIT = 96
+W_SPLIT = 80
 
 
 def tile_picked_densekindmix_none_p_kernel(
@@ -53,10 +53,17 @@ def tile_picked_densekindmix_none_p_kernel(
         nc.gpsimd.memset(ds_table[:].bitcast(I32), 0)
         nc.gpsimd.dma_start(ds_table[0:P:8, :].bitcast(I32), d_scales[0].bitcast(I32))
         nc.vector.memset(xs_table[:].bitcast(I32), 0)
-        nc.vector.memset(ds_plane[:].bitcast(I32), 0)
+        last = PACK - 1
+        tab_t = [new([P, 2 * J], F32, "tab%d" % t) for t in range(PREGATHERED)]
         hneg = [new([P, 2 * S], F32, "hneg%d" % t) for t in range(PACK)]
-        for t in range(PACK):
-            (nc.vector if t < 2 else nc.gpsimd).memset(hneg[t][:, S:], 0.0)
+        y = [new([P, 2 * S], F32, "y%d" % t) for t in range(last)] + [new([P, S], F32, "y%d" % last)]
+        for tile in tab_t + hneg[:1]:
+            nc.vector.memset(tile[:, S:], 0.0)
+        nc.vector.memset(ds_plane[:].bitcast(I32), 0)
+        for tile in hneg[2:]:
+            nc.gpsimd.memset(tile[:, S:], 0.0)
+        for tile in y[:last] + hneg[1:2]:
+            nc.scalar.activation(tile[:, S:], hneg[0][:, S:], COPY)
 
         tab_rows = tab.rearrange("(p t) j -> p t j", t=PACK)
         w_raw = new([P, PACK, H], F32, "w_raw")
@@ -68,7 +75,8 @@ def tile_picked_densekindmix_none_p_kernel(
             return tile
 
         n1_t = load_list(n1, "n1_t")
-        tab_t = [load_tab(t, "tab%d" % t) for t in range(2)]
+        for t in range(PREGATHERED):
+            nc.sync.dma_start(tab_t[t][:, :J], tab_rows[:, t, :])
         offs_t = load_list(offs, "offs_t")
         k1_t = load_list(k1, "k1_t")
         n2_t = load_list(n2, "n2_t")
@@ -88,8 +96,7 @@ def tile_picked_densekindmix_none_p_kernel(
 
         def pregather(t, tag):
             tab_picked.append(new([P, S], F32, "tab_picked%d" % t, tag=tag))
-            for c in range(2):
-                nc.vector.tensor_copy(tab_picked[t][:, half_cols(c)], tab_t[t][:].indirect(half_list(n1_t, c)))
+            nc.vector.tensor_copy(tab_picked[t][:], tab_t[t][:].indirect(n1_t[:]))
 
         pregather(0, "tab_picked0")
         xw_table = new([P, T], I32, "xw_table", tag="tab0")
@@ -117,7 +124,6 @@ def tile_picked_densekindmix_none_p_kernel(
         ds_picked = new([P, H], U8, "ds_picked", tag="tab0")
         nc.vector.tensor_copy(ds_picked[:], ds_table[:].indirect(k1_t[:]))
 
-        y = []
         for t in range(PACK):
             cols = slice(t * P, (t + 1) * P)
             acc = psum.tile([P, S], F32, name="y_acc%d" % t, tag="bank%d" % t)
@@ -130,46 +136,53 @@ def tile_picked_densekindmix_none_p_kernel(
                 start=True,
                 stop=True,
             )
-            y_t = new([P, S], F32, "y%d" % t)
-            nc.scalar.copy(y_t[:], acc[:])
-            y.append(y_t)
+            nc.scalar.copy(y[t][:, :S], acc[:])
 
         z_bf = [new([P, HALF, PACK], BF16, "z_bf%d" % c) for c in range(2)]
-        own = [[new([P, HALF], F32, "own%d_%d" % (t, c)) for c in range(2)] for t in range(PACK)]
-        other = [[new([P, HALF], F32, "other%d_%d" % (t, c)) for c in range(2)] for t in range(PACK)]
+        def places(c):
+            return slice(0, S) if c is None else half_cols(c)
 
-        def add_kind(t, c):
-            looked_up = tab_picked[t][:, half_cols(c)] if t < PREGATHERED else tab_t[t][:].indirect(half_list(n1_t, c))
-            nc.vector.tensor_tensor(own[t][c][:], looked_up, y[t][:, half_cols(c)], ALU.add)
+        def entries(tile, c):
+            return tile[:] if c is None else half_list(tile, c)
 
-        def fetch_other(t, c):
-            nc.vector.tensor_copy(other[t][c][:], y[t][:].indirect(half_list(n2_t, c)))
+        def stage_tiles(name):
+            whole = [new([P, S], F32, "%s%d" % (name, t)) for t in range(last)]
+            halves = [new([P, HALF], F32, "%s%d_%d" % (name, last, c)) for c in range(2)]
+            return lambda t, c: halves[c][:] if t == last else whole[t][:, places(c)]
 
-        def weigh_larger(t, c):
-            larger = new([P, HALF], F32, "larger%d_%d" % (t, c))
-            nc.vector.tensor_tensor(larger[:], own[t][c][:], other[t][c][:], ALU.max)
-            nc.scalar.activation(z_bf[c][:, :, t], larger[:], COPY, scale=gain[:, t : t + 1])
+        own, other, larger = stage_tiles("own"), stage_tiles("other"), stage_tiles("larger")
 
-        last = PACK - 1
-        for t in range(last):
-            for c in range(2):
-                add_kind(t, c)
-            if t == 0:
-                tab_t.append(load_tab(3, "tab_picked0"))
-                ds_dealt = new([P, H], U8, "ds_dealt")
-                nc.vector.tensor_copy(
-                    ds_dealt[:].bitcast(I32).rearrange("p (t a) -> p t a", t=PACK),
-                    ds_picked[:].bitcast(I32).rearrange("p (a t) -> p t a", t=PACK),
-                )
-                for q in range(4):
-                    nc.gpsimd.dma_start(
-                        ds_plane[32 * q : 32 * q + 4, :].bitcast(I32),
-                        ds_dealt[32 * q : 32 * q + 32 : 8, :].bitcast(I32),
-                    )
-            for c in range(2):
-                fetch_other(t, c)
-            for c in range(2):
-                weigh_larger(t, c)
+        def add_kind(t, c=None):
+            looked_up = tab_picked[t][:] if t < PREGATHERED else tab_t[t][:].indirect(entries(n1_t, c))
+            nc.vector.tensor_tensor(own(t, c), looked_up, y[t][:, places(c)], ALU.add)
+
+        def fetch_other(t, c=None):
+            nc.vector.tensor_copy(other(t, c), y[t][:].indirect(entries(n2_t, c)))
+
+        def weigh_larger(t, c=None):
+            nc.vector.tensor_tensor(larger(t, c), own(t, c), other(t, c), ALU.max)
+            for half in range(2) if c is None else [c]:
+                nc.scalar.activation(z_bf[half][:, :, t], larger(t, half), COPY, scale=gain[:, t : t + 1])
+
+        add_kind(0)
+        tab_t.append(load_tab(3, "tab_picked0"))
+        fetch_other(0)
+        ds_dealt = new([P, H], U8, "ds_dealt")
+        nc.vector.tensor_copy(
+            ds_dealt[:].bitcast(I32).rearrange("p (t a) -> p t a", t=PACK),
+            ds_picked[:].bitcast(I32).rearrange("p (a t) -> p t a", t=PACK),
+        )
+        for q in range(4):
+            nc.gpsimd.dma_start(
+                ds_plane[32 * q : 32 * q + 4, :].bitcast(I32), ds_dealt[32 * q : 32 * q + 32 : 8, :].bitcast(I32)
+            )
+        add_kind(1)
+        weigh_larger(0)
+        fetch_other(1)
+        add_kind(2, 0)
+        weigh_larger(1)
+        add_kind(2, 1)
+        fetch_other(2)
 
         z_codes = new([P, S], U32, "z_codes")
         z_plane = new([P, S], U8, "z_plane")
@@ -182,6 +195,7 @@ def tile_picked_densekindmix_none_p_kernel(
             )
 
         add_kind(last, 0)
+        weigh_larger(2)
         fetch_other(last, 0)
         add_kind(last, 1)
         weigh_larger(last, 0)
@@ -191,35 +205,35 @@ def tile_picked_densekindmix_none_p_kernel(
         weigh_larger(last, 1)
         nc.vector.tensor_copy(dw_picked[:, half_cols(1)], dw_table[:].bitcast(U32).indirect(half_list(k1_t, 1)))
         quantise_z(0)
-        dw_dealt = [new([P, P], U32, "dw_dealt0"), new([P, last * P], U32, "dw_dealt1")]
+        dw_dealt = [new([P, P], U32, "dw_dealt0")]
         dw_source = dw_picked[:].rearrange("p (a t b) -> p t a b", t=PACK, b=PACK)
         nc.vector.tensor_copy(dw_dealt[0][:].rearrange("p (a b) -> p a b", b=PACK), dw_source[:, 0])
         quantise_z(1)
+        dw_dealt.append(new([P, last * P], U32, "dw_dealt1", tag="z_bf1"))
         nc.vector.tensor_copy(dw_dealt[1][:].rearrange("p (t a b) -> p t a b", t=last, b=PACK), dw_source[:, 1:])
 
-        def second_product(t, places, bank):
+        def second_product(t, span, bank):
             cols = slice(t * P, (t + 1) * P)
-            acc = psum.tile([P, places.stop - places.start], F32, name="h_acc%d_%d" % (t, places.start), tag=bank)
+            acc = psum.tile([P, span.stop - span.start], F32, name="h_acc%d_%d" % (t, span.start), tag=bank)
             nc.tensor.matmul_mx(
                 out=acc[:],
                 lhsT=(dw_dealt[1][:, (t - 1) * P : t * P] if t else dw_dealt[0][:]).bitcast(FP8X4),
                 lhsT_scale=ds_plane[:, cols],
-                rhs=z_codes[:, places].bitcast(FP8X4),
-                rhs_scale=z_plane[:, places],
+                rhs=z_codes[:, span].bitcast(FP8X4),
+                rhs_scale=z_plane[:, span],
                 start=True,
                 stop=True,
             )
-            nc.scalar.activation(hneg[t][:, places], acc[:], COPY, scale=-0.0625)
+            nc.scalar.activation(hneg[t][:, span], acc[:], COPY, scale=-0.0625)
             return acc
 
-        hpos = [new([P, S], F32, "hpos%d" % t) for t in range(last)]
         for c in range(2):
             second_product(0, half_cols(c), "bank%d" % (PACK * (1 - c)))
+        hpos = [new([P, S], F32, "hpos%d" % t) for t in range(2)]
         nc.scalar.activation(hpos[0][:], hneg[0][:, :S], COPY, scale=-1.0)
-        for t in range(1, PACK):
-            acc = second_product(t, slice(0, S), "bank%d" % t)
-            if t < last:
-                nc.scalar.activation(hpos[t][:], acc[:], COPY, scale=0.0625)
+        nc.scalar.activation(hpos[1][:], second_product(1, slice(0, S), "bank1")[:], COPY, scale=0.0625)
+        for t in range(2, PACK):
+            second_product(t, slice(0, S), "bank%d" % t)
 
         out_rows = out.rearrange("(a t b) s -> t a b s", t=PACK, b=PACK)
 
@@ -235,9 +249,9 @@ def tile_picked_densekindmix_none_p_kernel(
             nc.scalar.copy(result[:], acc[:])
             return result
 
-        def fetch(t, lists, name, lo=0, hi=S):
-            tile = new([P, hi - lo], F32, "%s_%d_%d" % (name, t, lo))
-            nc.vector.tensor_copy(tile[:], hneg[t][:].indirect(lists[:, lo // 16 : hi // 16]))
+        def fetch(t, lists, name):
+            tile = new([P, S], F32, "%s_%d" % (name, t))
+            nc.vector.tensor_copy(tile[:], hneg[t][:].indirect(lists[:]))
             return tile
 
         def own_less(t, lists, name):
@@ -245,38 +259,37 @@ def tile_picked_densekindmix_none_p_kernel(
             nc.vector.tensor_tensor(tile[:], hneg[t][:].indirect(lists[:]), hpos[t][:], ALU.add)
             return tile
 
-        for t in range(last):
-            if t == 0:
-                at4 = fetch(t, n4_t, "at4")
-                at5 = fetch(t, n5_t, "at5")
-            else:
-                at4 = own_less(t, n4_t, "at4")
-                at5 = own_less(t, n5_t, "at5")
+        for t in range(2):
+            at4, at5 = [(own_less if t else fetch)(t, lists, name) for lists, name in ((n4_t, "at4"), (n5_t, "at5"))]
             drop = own_less(t, n3_t, "drop")
             far = new([P, S], F32, "far%d" % t)
             nc.vector.tensor_tensor(far[:], at4[:], at5[:], ALU.min)
-            rise = new([P, S], F32, "rise%d" % t, tag="turned%d_sb" % (t - 1) if t else None)
+            rise = new([P, S], F32, "rise%d" % t)
             nc.scalar.activation(rise[:], drop[:], RELU, scale=-1.0)
-            turned = turned_sum([far, rise] if t else [hpos[t], far, rise], "turned%d" % t, "bank%d" % (5 + t % 2))
-            nc.sync.dma_start(out_rows[t], turned_sum([turned], "res%d" % t, "bank7")[:])
+            turned = turned_sum([far, rise] if t else [hpos[t], far, rise], "turned%d" % t, "bank%d" % (5 + t))
+            nc.scalar.dma_start(out_rows[t], turned_sum([turned], "back%d" % t, "bank%d" % (7 - 3 * t))[:])
 
-        at3 = [fetch(last, n3_t, "at3", c * HALF, (c + 1) * HALF) for c in range(2)]
         near, via4, via5, res = [
-            [new([P, HALF], F32, "%s_last%d" % (name, c)) for c in range(2)] for name in ("near", "via4", "via5", "res")
+            {t: new([P, S], F32, "%s_%d" % (name, t)) for t in (2, 3)} for name in ("near", "via4", "via5", "res")
         ]
 
-        def less_near(dst, lists, c):
-            nc.vector.tensor_tensor(dst[c][:], hneg[last][:].indirect(half_list(lists, c)), near[c][:], ALU.subtract)
+        def less_near(dst, lists, t, c=None):
+            nc.vector.tensor_tensor(
+                dst[t][:, places(c)], hneg[t][:].indirect(entries(lists, c)), near[t][:, places(c)], ALU.subtract
+            )
 
-        def finish(c):
-            nc.vector.tensor_tensor(res[c][:], via4[c][:], via5[c][:], ALU.min)
-            nc.sync.dma_start(out_rows[last][:, :, half_cols(c)], res[c][:])
+        def finish(t, c=None):
+            nc.vector.tensor_tensor(res[t][:, places(c)], via4[t][:, places(c)], via5[t][:, places(c)], ALU.min)
+            nc.sync.dma_start(out_rows[t][:, :, places(c)], res[t][:, places(c)])
 
-        for c in range(2):
-            nc.vector.tensor_tensor(near[c][:], hneg[last][:, half_cols(c)], at3[c][:], ALU.min)
-        less_near(via4, n4_t, 0)
-        less_near(via5, n5_t, 0)
-        less_near(via4, n4_t, 1)
-        finish(0)
-        less_near(via5, n5_t, 1)
-        finish(1)
+        at3 = {t: fetch(t, n3_t, "at3") for t in (2, 3)}
+        for t in (2, 3):
+            nc.vector.tensor_tensor(near[t][:], hneg[t][:, :S], at3[t][:], ALU.min)
+        for t in (2, 3):
+            less_near(via4, n4_t, t)
+        less_near(via5, n5_t, 2)
+        less_near(via5, n5_t, 3, 0)
+        finish(2)
+        finish(3, 0)
+        less_near(via5, n5_t, 3, 1)
+        finish(3, 1)

from contextlib import ExitStack

import concourse.mybir as mybir
from concourse.masks import make_identity

K, T, S, H, J, G = 512, 2048, 512, 512, 512, 2048
FLOPS = 2 * K * H * S + 2 * K * H * S

F32 = mybir.dt.float32
BF16 = mybir.dt.bfloat16
I32 = mybir.dt.int32
U32 = mybir.dt.uint32
U16 = mybir.dt.uint16
U8 = mybir.dt.uint8
FP8X4 = mybir.dt.float8_e4m3fn_x4
ALU = mybir.AluOpType
COPY = mybir.ActivationFunctionType.Copy
RELU = mybir.ActivationFunctionType.Relu

P = 128
PACK = 4
HALF = S // 2
LIST_COLS = S // 16
PREGATHERED = 2
W_SPLIT = 80


def tile_picked_densekindmix_none_p_kernel(
    tc, x_words, x_scales, w1, tab, gs, d_words, d_scales, offs, n1, n2, k1, n3, n4, n5, out
):
    nc = tc.nc
    with ExitStack() as ctx:
        keep = ctx.enter_context(tc.tile_pool(name="keep", bufs=1))
        psum = ctx.enter_context(tc.psum_pool(name="psum", bufs=1))

        def new(shape, dtype, name, tag=None):
            return keep.tile(shape, dtype, name=name, tag=tag or name, align_bytes=64)

        def load_list(src, name):
            tile = new([P, LIST_COLS], U16, name)
            nc.sync.dma_start(tile[:], src)
            return tile

        def half_cols(c):
            return slice(c * HALF, (c + 1) * HALF)

        def half_list(tile, c):
            return tile[:, c * LIST_COLS // 2 : (c + 1) * LIST_COLS // 2]

        ds_table = new([P, G], U8, "ds_table")
        xs_table = new([P, T], U8, "xs_table")
        ds_plane = new([P, H], U8, "ds_plane")
        nc.gpsimd.memset(ds_table[:].bitcast(I32), 0)
        nc.gpsimd.dma_start(ds_table[0:P:8, :].bitcast(I32), d_scales[0].bitcast(I32))
        nc.vector.memset(xs_table[:].bitcast(I32), 0)
        last = PACK - 1
        tab_t = [new([P, 2 * J], F32, "tab%d" % t) for t in range(PREGATHERED)]
        hneg = [new([P, 2 * S], F32, "hneg%d" % t) for t in range(PACK)]
        y = [new([P, 2 * S], F32, "y%d" % t) for t in range(last)] + [new([P, S], F32, "y%d" % last)]
        for tile in tab_t + hneg[:1]:
            nc.vector.memset(tile[:, S:], 0.0)
        nc.vector.memset(ds_plane[:].bitcast(I32), 0)
        for tile in hneg[2:]:
            nc.gpsimd.memset(tile[:, S:], 0.0)
        for tile in y[:last] + hneg[1:2]:
            nc.scalar.activation(tile[:, S:], hneg[0][:, S:], COPY)

        tab_rows = tab.rearrange("(p t) j -> p t j", t=PACK)
        w_raw = new([P, PACK, H], F32, "w_raw")
        gain = new([P, PACK], F32, "gain")

        def load_tab(t, tag):
            tile = new([P, J], F32, "tab%d" % t, tag=tag)
            nc.sync.dma_start(tile[:], tab_rows[:, t, :])
            return tile

        n1_t = load_list(n1, "n1_t")
        for t in range(PREGATHERED):
            nc.sync.dma_start(tab_t[t][:, :J], tab_rows[:, t, :])
        offs_t = load_list(offs, "offs_t")
        k1_t = load_list(k1, "k1_t")
        n2_t = load_list(n2, "n2_t")
        n3_t = load_list(n3, "n3_t")
        nc.sync.dma_start(w_raw[:], w1.rearrange("(p j) c -> p j c", j=PACK))
        n4_t = load_list(n4, "n4_t")
        n5_t = load_list(n5, "n5_t")
        for q in range(4):
            nc.sync.dma_start(
                xs_table[32 * q : 32 * q + 4, :].bitcast(I32), x_scales[0, 4 * q : 4 * q + 4, :].bitcast(I32)
            )
        nc.gpsimd.dma_start(gain[:], gs.rearrange("(p t) o -> p (t o)", t=PACK))
        ident = new([P, P], F32, "ident")
        make_identity(nc, ident[:])

        tab_picked = []

        def pregather(t, tag):
            tab_picked.append(new([P, S], F32, "tab_picked%d" % t, tag=tag))
            nc.vector.tensor_copy(tab_picked[t][:], tab_t[t][:].indirect(n1_t[:]))

        pregather(0, "tab_picked0")
        xw_table = new([P, T], I32, "xw_table", tag="tab0")
        nc.sync.dma_start(xw_table[:], x_words[0].rearrange("p n t -> p (n t)").bitcast(I32))

        pregather(1, "tab_picked1")
        tab_t.append(load_tab(2, "tab1"))
        w_bf = new([P, H * PACK], BF16, "w_bf")
        w_dealt = w_bf[:].rearrange("p (t m j) -> p m t j", t=PACK, j=PACK)
        w_source = w_raw[:].rearrange("p j (m t) -> p m t j", t=PACK)
        nc.scalar.activation(w_dealt[:, :W_SPLIT], w_source[:, :W_SPLIT], COPY)
        nc.vector.tensor_copy(w_dealt[:, W_SPLIT:], w_source[:, W_SPLIT:])
        dw_table = new([P, G], I32, "dw_table", tag="w_raw")
        nc.sync.dma_start(dw_table[:], d_words[0].rearrange("p n t -> p (n t)").bitcast(I32))
        xs_picked = new([P, S], U8, "xs_picked")
        nc.vector.tensor_copy(xs_picked[:], xs_table[:].indirect(offs_t[:]))

        w_codes = new([P, H], U32, "w_codes", tag="xs_table")
        w_plane = new([P, H], U8, "w_plane")
        nc.vector.quantize_mx(out=w_codes[:].bitcast(FP8X4), scales=w_plane[:], in_=w_bf[:])

        xw_picked = new([P, S], U32, "xw_picked", tag="w_bf")
        nc.vector.tensor_copy(xw_picked[:], xw_table[:].bitcast(U32).indirect(offs_t[:]))

        ds_picked = new([P, H], U8, "ds_picked", tag="tab0")
        nc.vector.tensor_copy(ds_picked[:], ds_table[:].indirect(k1_t[:]))

        for t in range(PACK):
            cols = slice(t * P, (t + 1) * P)
            acc = psum.tile([P, S], F32, name="y_acc%d" % t, tag="bank%d" % t)
            nc.tensor.matmul_mx(
                out=acc[:],
                lhsT=w_codes[:, cols].bitcast(FP8X4),
                lhsT_scale=w_plane[:, cols],
                rhs=xw_picked[:].bitcast(FP8X4),
                rhs_scale=xs_picked[:],
                start=True,
                stop=True,
            )
            nc.scalar.copy(y[t][:, :S], acc[:])

        z_bf = [new([P, HALF, PACK], BF16, "z_bf%d" % c) for c in range(2)]
        def places(c):
            return slice(0, S) if c is None else half_cols(c)

        def entries(tile, c):
            return tile[:] if c is None else half_list(tile, c)

        def stage_tiles(name):
            whole = [new([P, S], F32, "%s%d" % (name, t)) for t in range(last)]
            halves = [new([P, HALF], F32, "%s%d_%d" % (name, last, c)) for c in range(2)]
            return lambda t, c: halves[c][:] if t == last else whole[t][:, places(c)]

        own, other, larger = stage_tiles("own"), stage_tiles("other"), stage_tiles("larger")

        def add_kind(t, c=None):
            looked_up = tab_picked[t][:] if t < PREGATHERED else tab_t[t][:].indirect(entries(n1_t, c))
            nc.vector.tensor_tensor(own(t, c), looked_up, y[t][:, places(c)], ALU.add)

        def fetch_other(t, c=None):
            nc.vector.tensor_copy(other(t, c), y[t][:].indirect(entries(n2_t, c)))

        def weigh_larger(t, c=None):
            nc.vector.tensor_tensor(larger(t, c), own(t, c), other(t, c), ALU.max)
            for half in range(2) if c is None else [c]:
                nc.scalar.activation(z_bf[half][:, :, t], larger(t, half), COPY, scale=gain[:, t : t + 1])

        add_kind(0)
        tab_t.append(load_tab(3, "tab_picked0"))
        fetch_other(0)
        ds_dealt = new([P, H], U8, "ds_dealt")
        nc.vector.tensor_copy(
            ds_dealt[:].bitcast(I32).rearrange("p (t a) -> p t a", t=PACK),
            ds_picked[:].bitcast(I32).rearrange("p (a t) -> p t a", t=PACK),
        )
        for q in range(4):
            nc.gpsimd.dma_start(
                ds_plane[32 * q : 32 * q + 4, :].bitcast(I32), ds_dealt[32 * q : 32 * q + 32 : 8, :].bitcast(I32)
            )
        add_kind(1)
        weigh_larger(0)
        fetch_other(1)
        add_kind(2, 0)
        weigh_larger(1)
        add_kind(2, 1)
        fetch_other(2)

        z_codes = new([P, S], U32, "z_codes")
        z_plane = new([P, S], U8, "z_plane")

        def quantise_z(c):
            nc.vector.quantize_mx(
                out=z_codes[:, half_cols(c)].bitcast(FP8X4),
                scales=z_plane[:, half_cols(c)],
                in_=z_bf[c][:].rearrange("p s t -> p (s t)"),
            )

        add_kind(last, 0)
        weigh_larger(2)
        fetch_other(last, 0)
        add_kind(last, 1)
        weigh_larger(last, 0)
        fetch_other(last, 1)
        dw_picked = new([P, H], U32, "dw_picked", tag="other%d_%d" % (last, 0))
        nc.vector.tensor_copy(dw_picked[:, half_cols(0)], dw_table[:].bitcast(U32).indirect(half_list(k1_t, 0)))
        weigh_larger(last, 1)
        nc.vector.tensor_copy(dw_picked[:, half_cols(1)], dw_table[:].bitcast(U32).indirect(half_list(k1_t, 1)))
        quantise_z(0)
        dw_dealt = [new([P, P], U32, "dw_dealt0")]
        dw_source = dw_picked[:].rearrange("p (a t b) -> p t a b", t=PACK, b=PACK)
        nc.vector.tensor_copy(dw_dealt[0][:].rearrange("p (a b) -> p a b", b=PACK), dw_source[:, 0])
        quantise_z(1)
        dw_dealt.append(new([P, last * P], U32, "dw_dealt1", tag="z_bf1"))
        nc.vector.tensor_copy(dw_dealt[1][:].rearrange("p (t a b) -> p t a b", t=last, b=PACK), dw_source[:, 1:])

        def second_product(t, span, bank):
            cols = slice(t * P, (t + 1) * P)
            acc = psum.tile([P, span.stop - span.start], F32, name="h_acc%d_%d" % (t, span.start), tag=bank)
            nc.tensor.matmul_mx(
                out=acc[:],
                lhsT=(dw_dealt[1][:, (t - 1) * P : t * P] if t else dw_dealt[0][:]).bitcast(FP8X4),
                lhsT_scale=ds_plane[:, cols],
                rhs=z_codes[:, span].bitcast(FP8X4),
                rhs_scale=z_plane[:, span],
                start=True,
                stop=True,
            )
            nc.scalar.activation(hneg[t][:, span], acc[:], COPY, scale=-0.0625)
            return acc

        for c in range(2):
            second_product(0, half_cols(c), "bank%d" % (PACK * (1 - c)))
        hpos = [new([P, S], F32, "hpos%d" % t) for t in range(2)]
        nc.scalar.activation(hpos[0][:], hneg[0][:, :S], COPY, scale=-1.0)
        nc.scalar.activation(hpos[1][:], second_product(1, slice(0, S), "bank1")[:], COPY, scale=0.0625)
        for t in range(2, PACK):
            second_product(t, slice(0, S), "bank%d" % t)

        out_rows = out.rearrange("(a t b) s -> t a b s", t=PACK, b=PACK)

        def turned_sum(terms, name, bank):
            acc = psum.tile([P, S], F32, name=name, tag=bank)
            for b in range(S // P):
                block = slice(b * P, (b + 1) * P)
                for i, term in enumerate(terms):
                    nc.tensor.matmul(
                        acc[:, block], term[:, block], ident[:], start=i == 0, stop=i == len(terms) - 1, is_transpose=True
                    )
            result = new([P, S], F32, name + "_sb")
            nc.scalar.copy(result[:], acc[:])
            return result

        def fetch(t, lists, name):
            tile = new([P, S], F32, "%s_%d" % (name, t))
            nc.vector.tensor_copy(tile[:], hneg[t][:].indirect(lists[:]))
            return tile

        def own_less(t, lists, name):
            tile = new([P, S], F32, "%s_%d" % (name, t))
            nc.vector.tensor_tensor(tile[:], hneg[t][:].indirect(lists[:]), hpos[t][:], ALU.add)
            return tile

        for t in range(2):
            at4, at5 = [(own_less if t else fetch)(t, lists, name) for lists, name in ((n4_t, "at4"), (n5_t, "at5"))]
            drop = own_less(t, n3_t, "drop")
            far = new([P, S], F32, "far%d" % t)
            nc.vector.tensor_tensor(far[:], at4[:], at5[:], ALU.min)
            rise = new([P, S], F32, "rise%d" % t)
            nc.scalar.activation(rise[:], drop[:], RELU, scale=-1.0)
            turned = turned_sum([far, rise] if t else [hpos[t], far, rise], "turned%d" % t, "bank%d" % (5 + t))
            nc.scalar.dma_start(out_rows[t], turned_sum([turned], "back%d" % t, "bank%d" % (7 - 3 * t))[:])

        near, via4, via5, res = [
            {t: new([P, S], F32, "%s_%d" % (name, t)) for t in (2, 3)} for name in ("near", "via4", "via5", "res")
        ]

        def less_near(dst, lists, t, c=None):
            nc.vector.tensor_tensor(
                dst[t][:, places(c)], hneg[t][:].indirect(entries(lists, c)), near[t][:, places(c)], ALU.subtract
            )

        def finish(t, c=None):
            nc.vector.tensor_tensor(res[t][:, places(c)], via4[t][:, places(c)], via5[t][:, places(c)], ALU.min)
            nc.sync.dma_start(out_rows[t][:, :, places(c)], res[t][:, places(c)])

        at3 = {t: fetch(t, n3_t, "at3") for t in (2, 3)}
        for t in (2, 3):
            nc.vector.tensor_tensor(near[t][:], hneg[t][:, :S], at3[t][:], ALU.min)
        for t in (2, 3):
            less_near(via4, n4_t, t)
        less_near(via5, n5_t, 2)
        less_near(via5, n5_t, 3, 0)
        finish(2)
        finish(3, 0)
        less_near(via5, n5_t, 3, 1)
        finish(3, 1)
